import numpy as np
import ml_dtypes


def mxq(x, axis, fmt="e4m3"):
    dtype, down = {"e4m3": (ml_dtypes.float8_e4m3fn, 7), "e5m2": (ml_dtypes.float8_e5m2, 14)}[fmt]
    v = np.moveaxis(np.asarray(x, np.float32).astype(ml_dtypes.bfloat16).astype(np.float64), axis, -1)
    blocks = v.reshape(v.shape[:-1] + (-1, 32))
    amax = np.abs(blocks).max(-1, keepdims=True)
    byte = np.maximum(np.where(amax > 0, np.frexp(amax)[1] - 1 + 127, 0) - down, 1)
    scale = np.exp2(byte - 127.0)
    codes = (blocks / scale).astype(np.float32).astype(dtype).astype(np.float64)
    return np.moveaxis((codes * scale).reshape(v.shape), -1, axis)


WIDE = False


def mx_kscale(k):
    if not WIDE:
        return np.ones(k)
    levels = np.array([10, -10, 5, -5, 0])
    if k % 512:
        return np.exp2(np.random.permutation(np.resize(levels, k // 32))).repeat(32)
    a = np.empty((k // 512, 16))
    for p in range(k // 512):
        a[p, :8] = np.random.permutation(np.resize(levels, 8))
        for g in range(8):
            far = levels[np.abs(levels - a[p, g]) >= 10]
            a[p, g + 8] = far[np.random.randint(len(far))]
    return np.exp2(a.ravel()).repeat(32)


def f64(x):
    return np.asarray(x).astype(np.float64)


def striped(idx):
    return np.tile(idx.reshape(-1, 16).T, (8, 1)).astype(np.uint16)


def unstriped(offs):
    return offs[:16].T.reshape(-1).astype(np.int64)


def striped8(idx):
    return np.concatenate([x.reshape(-1, 16).T for x in idx]).astype(np.uint16)


def runs(offs, k):
    lists = np.stack([offs[16 * r : 16 * r + 16].T.reshape(-1) for r in range(8)]).astype(np.int64)
    return lists[np.arange(k) % 512 // 64]


def pack_weight(w):
    k, n = w.shape
    w = f64(np.asarray(w, np.float32).astype(ml_dtypes.bfloat16)).reshape(k // 32, 32, n)
    amax = np.abs(w).max(1)
    byte = np.clip(np.where(amax > 0, np.frexp(amax)[1] - 1 + 127 - 7, 1), 1, 254)
    scaled = (w * np.exp2(127.0 - byte)[:, None, :]).reshape(k, n).astype(np.float32)
    words = np.ascontiguousarray(scaled.reshape(k // 512, 128, 4, n).transpose(0, 1, 3, 2)).astype(ml_dtypes.float8_e4m3fn).view(np.uint8)
    return words, np.ascontiguousarray(byte.astype(np.uint8).reshape(k // 512, 16, n))


def unpack_weight(words, scales):
    g, p, n, _ = words.shape
    vals = np.ascontiguousarray(words).view(ml_dtypes.float8_e4m3fn).astype(np.float64) * np.repeat(np.exp2(scales.astype(np.float64) - 127.0), 8, axis=1)[..., None]
    return vals.transpose(0, 1, 3, 2).reshape(g * 512, n)


def sigmoid(v):
    return 1.0 / (1.0 + np.exp(-np.maximum(v, -700.0)))


K, T, S, H, G, U = 512, 2048, 256, 512, 2048, 512


def setup_inputs():
    n = np.random.standard_normal
    s = mx_kscale(K)[:, None]
    packed_xT = pack_weight(n((K, T)) * s)
    packed_dT = pack_weight(n((K, G)) / s)
    perm = np.random.permutation(U)
    return {
        "x_words": packed_xT[0],
        "x_scales": packed_xT[1],
        "w1": (n((K, H)) / np.sqrt(K) / s).astype(np.float32),
        "sl": np.random.uniform(1.0, 2.0, (H, 1)).astype(np.float32),
        "th": (0.5 * n((H, 1))).astype(np.float32),
        "gs": (np.random.uniform(0.5, 1.5, (K, 1)) * s).astype(np.float32),
        "d_words": packed_dT[0],
        "d_scales": packed_dT[1],
        "offs": striped8(np.random.randint(0, T, (8, S))),
        "n1": striped8(np.stack([np.random.permutation(S) for _ in range(8)])),
        "n2": striped8(np.stack([np.random.permutation(S) for _ in range(8)])),
        "k1": striped8(np.random.randint(0, G, (8, H))),
        "n3": striped(perm[:S]),
        "n4": striped(perm[S:]),
        "n5": striped(np.random.permutation(U)),
    }


def reference(x_words, x_scales, w1, sl, th, gs, d_words, d_scales, offs, n1, n2, k1, n3, n4, n5):
    d_k1 = unpack_weight(d_words, d_scales)[np.arange(K)[:, None], runs(k1, K)]
    xq = unpack_weight(x_words, x_scales)[np.arange(K)[:, None], runs(offs, K)]
    y = mxq(f64(w1), 0, "e4m3").T @ xq
    sg = sigmoid(f64(sl) * (y[np.arange(H)[:, None], runs(n1, H)] - f64(th)))
    st = y * sg
    z = f64(gs) * (st - (0.5 * (st[np.arange(H)[:, None], runs(n2, H)])))
    h = 0.0625 * ((d_k1.T @ mxq(z, 0, "e4m3")))
    nw = 0.5 * h
    ph = np.zeros((H, U))
    ph[:, unstriped(n3)] = h
    pg = ph.copy()
    pg[:, unstriped(n4)] = nw
    return pg - pg[:, unstriped(n5)]

@@ -1,0 +1,179 @@
+from contextlib import ExitStack
+
+import concourse.mybir as mybir
+
+F32 = mybir.dt.float32
+BF16 = mybir.dt.bfloat16
+I32 = mybir.dt.int32
+U32 = mybir.dt.uint32
+U16 = mybir.dt.uint16
+U8 = mybir.dt.uint8
+FP8X4 = mybir.dt.float8_e4m3fn_x4
+ALU = mybir.AluOpType
+ACT = mybir.ActivationFunctionType
+
+K, T, S, H, U = 512, 2048, 256, 512, 512
+P = 128
+PACK = 4
+FLOPS = 2 * K * H * S * 2
+
+CHUNKS = ((0, 64), (64, 128), (128, 256))
+
+
+def offsets(lst, lo, hi):
+    return lst[:, lo // 16 : hi // 16]
+
+
+def tile_picked_hdenseehppagtwo_none_p_kernel(
+    tc, x_words, x_scales, w1, sl, th, gs, d_words, d_scales, offs, n1, n2, k1, n3, n4, n5, out
+):
+    nc = tc.nc
+    with ExitStack() as ctx:
+        keep = ctx.enter_context(tc.tile_pool(name="keep", bufs=1))
+        psum = ctx.enter_context(tc.psum_pool(name="psum", bufs=1))
+
+        def load_list(name, src):
+            lst = keep.tile(list(src.shape), U16, name=name)
+            nc.sync.dma_start(lst[:], src)
+            return lst
+
+        def load_rows(name, src, queue):
+            col = keep.tile([P, PACK], F32, name=name)
+            queue.dma_start(col[:], src.rearrange("(p t) o -> p (t o)", t=PACK))
+            return col
+
+        def load_words(tag, src):
+            words = keep.tile([P, T], I32, tag=tag, align_bytes=64)
+            nc.sync.dma_start(words[:], src[0].rearrange("p n r -> p (n r)").bitcast(I32))
+            return words
+
+        def pick_scales(name, rows, lst, n):
+            picked = keep.tile([P, n], U8, name=name + "_picked")
+            nc.vector.tensor_copy(picked[:], rows[:].indirect(lst[:]))
+            return picked
+
+        def move_rows(plane, picked):
+            for a in range(1, 4):
+                nc.sync.dma_start(plane[a:P:32, :].bitcast(I32), picked[8 * a : P : 32, :].bitcast(I32))
+
+        offs_l = load_list("offs_l", offs)
+        x_rows = keep.tile([P, T], U8, tag="x_rows_then_words", align_bytes=64)
+        nc.sync.dma_start(x_rows[:].bitcast(I32), x_scales[0].bitcast(I32).unsqueeze(1).to_broadcast([16, 8, T // 4]))
+        d_rows = keep.tile([P, T], U8, tag="d_rows_words_z", align_bytes=64)
+        nc.vector.memset(d_rows[:].bitcast(I32), 0)
+        nc.sync.dma_start(d_rows[0:P:8, :].bitcast(I32), d_scales[0].bitcast(I32))
+        k1_l = load_list("k1_l", k1)
+        n1_l = load_list("n1_l", n1)
+        n2_l = load_list("n2_l", n2)
+        n3_l = load_list("n3_l", n3)
+        w_raw = keep.tile([P, PACK, H], F32)
+        nc.sync.dma_start(w_raw[:], w1.rearrange("(p j) c -> p j c", j=PACK))
+        n4_l = load_list("n4_l", n4)
+        n5_l = load_list("n5_l", n5)
+        sl_c = load_rows("sl_c", sl, nc.gpsimd)
+        th_c = load_rows("th_c", th, nc.gpsimd)
+        gs_c = load_rows("gs_c", gs, nc.gpsimd)
+
+        x_plane = keep.tile([P, S], U8, align_bytes=64)
+        nc.vector.memset(x_plane[:].bitcast(I32), 0)
+        x_picked = pick_scales("x", x_rows, offs_l, S)
+        move_rows(x_plane, x_picked)
+        x_table = load_words("x_rows_then_words", x_words)
+        for q in range(0, P, 32):
+            nc.vector.tensor_copy(x_plane[q : q + 1, :].bitcast(I32), x_picked[q : q + 1, :].bitcast(I32))
+        d_picked = pick_scales("d", d_rows, k1_l, H)
+        d_table = load_words("d_rows_words_z", d_words)
+        d_plane = keep.tile([P, H], U8, align_bytes=64)
+        nc.vector.tensor_copy(d_plane[:].bitcast(I32), d_picked[:].bitcast(I32))
+        move_rows(d_plane, d_picked)
+
+        w_bf = keep.tile([P, PACK, P, PACK], BF16, align_bytes=64)
+        w_to = w_bf[:].rearrange("p t m j -> p m j t")
+        w_from = w_raw[:].rearrange("p j (m t) -> p m j t", t=PACK)
+        nc.vector.tensor_copy(w_to[:, 0:64], w_from[:, 0:64])
+        nc.scalar.copy(w_to[:, 64:P], w_from[:, 64:P])
+        w_codes = keep.tile([P, H], U32, align_bytes=64)
+        w_plane = keep.tile([P, H], U8, align_bytes=64)
+        nc.vector.quantize_mx(w_codes[:].bitcast(FP8X4), w_plane[:], w_bf[:].rearrange("p t m j -> p (t m j)"))
+
+        x_codes = keep.tile([P, S], U32, align_bytes=64)
+        nc.vector.tensor_copy(x_codes[:], x_table[:].bitcast(U32).indirect(offs_l[:]))
+
+        bias_c = keep.tile([P, PACK], F32)
+        nc.vector.scalar_tensor_tensor(bias_c[:], sl_c[:], -1.0, th_c[:], ALU.mult, ALU.mult)
+
+        u = keep.tile([P, PACK, S], F32)
+        for t in range(PACK):
+            cols = slice(P * t, P * (t + 1))
+            y_ps = psum.tile([P, S], F32, name=f"bank{t}")
+            nc.tensor.matmul_mx(
+                y_ps[:], lhsT=w_codes[:, cols].bitcast(FP8X4), lhsT_scale=w_plane[:, cols],
+                rhs=x_codes[:].bitcast(FP8X4), rhs_scale=x_plane[:], start=True, stop=True,
+            )
+            y = keep.tile([P, S], F32, tag=f"y{t}")
+            nc.vector.tensor_copy(y[:], y_ps[:])
+            sg = keep.tile([P, S], F32, tag=f"sg{t}")
+            for lo in (0, S // 2):
+                nc.scalar.activation(
+                    sg[:, lo : lo + S // 2], y[:].indirect(offsets(n1_l, lo, lo + S // 2)), ACT.Sigmoid,
+                    bias=bias_c[:, t : t + 1], scale=sl_c[:, t : t + 1],
+                )
+            nc.vector.scalar_tensor_tensor(u[:, t, :], y[:], gs_c[:, t : t + 1], sg[:], ALU.mult, ALU.mult)
+
+        d_codes = keep.tile([P, H], U32, align_bytes=64)
+        for lo in (0, H // 2):
+            nc.vector.tensor_copy(
+                d_codes[:, lo : lo + H // 2], d_table[:].bitcast(U32).indirect(offsets(k1_l, lo, lo + H // 2))
+            )
+
+        h = [keep.tile([P, S], F32, name=f"h{m}") for m in range(H // P)]
+        for c, (lo, hi) in enumerate(CHUNKS):
+            width = hi - lo
+            half = keep.tile([P, PACK, width], F32, tag=("half0", "sg3", "y3")[c])
+            for s in range(lo, hi, 64):
+                for t in range(PACK):
+                    nc.scalar.activation(
+                        half[:, t, s - lo : s - lo + 64], u[:, t, :].indirect(offsets(n2_l, s, s + 64)), ACT.Copy, scale=0.5
+                    )
+            z = keep.tile([P, width, PACK], BF16, tag="d_rows_words_z", align_bytes=64)
+            nc.vector.tensor_tensor(
+                z[:].rearrange("p (a i) t -> p a t i", i=4),
+                u[:, :, lo:hi].rearrange("p t (a i) -> p a t i", i=4),
+                half[:].rearrange("p t (a i) -> p a t i", i=4),
+                ALU.subtract,
+            )
+            z_codes = keep.tile([P, width], U32, name=f"z_codes{c}", align_bytes=64)
+            z_plane = keep.tile([P, width], U8, name=f"z_plane{c}", align_bytes=64)
+            nc.vector.quantize_mx(z_codes[:].bitcast(FP8X4), z_plane[:], z[:].rearrange("p j t -> p (j t)"))
+            for m in range(H // P):
+                cols = slice(P * m, P * (m + 1))
+                h_ps = psum.tile([P, width], F32, name=f"bank{(4 * (c + 1) + m) % 8}")
+                nc.tensor.matmul_mx(
+                    h_ps[:], lhsT=d_codes[:, cols].bitcast(FP8X4), lhsT_scale=d_plane[:, cols],
+                    rhs=z_codes[:].bitcast(FP8X4), rhs_scale=z_plane[:], start=True, stop=True,
+                )
+                nc.vector.tensor_scalar(h[m][:, lo:hi], h_ps[:], 0.0625, None, ALU.mult)
+
+        page = [keep.tile([P, U], F32, name=f"page{m}") for m in range(H // P)]
+
+        def put(pair, lo, hi):
+            for lst, factor in ((n3_l, 1.0), (n4_l, 0.5)):
+                for m in pair:
+                    nc.scalar.activation(page[m][:].indirect(offsets(lst, lo, hi)), h[m][:, lo:hi], ACT.Copy, scale=factor)
+
+        def finish(m):
+            for lo in (0, U // 2):
+                hi = lo + U // 2
+                other = keep.tile([P, U // 2], F32, name=f"other{m}_{lo}")
+                nc.scalar.activation(other[:], page[m][:].indirect(offsets(n5_l, lo, hi)), ACT.Copy)
+                res = keep.tile([P, U // 2], F32, name=f"res{m}_{lo}")
+                nc.vector.tensor_tensor(res[:], page[m][:, lo:hi], other[:], ALU.subtract)
+                nc.sync.dma_start(out[P * m : P * (m + 1), lo:hi], res[:])
+
+        first = CHUNKS[0][1]
+        for pair in ((0, 1), (2, 3)):
+            put(pair, 0, first)
+        for pair in ((0, 1), (2, 3)):
+            put(pair, first, S)
+            for m in pair:
+                finish(m)

@@ -17,6 +17,8 @@ P = 128
 PACK = 4
 FLOPS = 2 * K * H * S * 2
 
+LAST = 352
+W_SPLIT = 80
 CHUNKS = ((0, 64), (64, 128), (128, 256))
 
 
@@ -50,48 +52,43 @@ def tile_picked_hdenseehppagtwo_none_p_kernel(
         def pick_scales(name, rows, lst, n):
             picked = keep.tile([P, n], U8, name=name + "_picked")
             nc.vector.tensor_copy(picked[:], rows[:].indirect(lst[:]))
-            return picked
-
-        def move_rows(plane, picked):
+            plane = keep.tile([P, n], U8, name=name + "_plane", align_bytes=64)
+            nc.vector.tensor_copy(plane[:].bitcast(I32), picked[:].bitcast(I32))
             for a in range(1, 4):
                 nc.sync.dma_start(plane[a:P:32, :].bitcast(I32), picked[8 * a : P : 32, :].bitcast(I32))
+            return plane
 
         offs_l = load_list("offs_l", offs)
-        x_rows = keep.tile([P, T], U8, tag="x_rows_then_words", align_bytes=64)
+        x_rows = keep.tile([P, T], U8)
         nc.sync.dma_start(x_rows[:].bitcast(I32), x_scales[0].bitcast(I32).unsqueeze(1).to_broadcast([16, 8, T // 4]))
         d_rows = keep.tile([P, T], U8, tag="d_rows_words_z", align_bytes=64)
-        nc.vector.memset(d_rows[:].bitcast(I32), 0)
+        nc.vector.memset(d_rows[:, 0 : T // 2].bitcast(I32), 0)
+        nc.gpsimd.memset(d_rows[:, T // 2 : T].bitcast(I32), 0)
         nc.sync.dma_start(d_rows[0:P:8, :].bitcast(I32), d_scales[0].bitcast(I32))
         k1_l = load_list("k1_l", k1)
+        sl_c = load_rows("sl_c", sl, nc.sync)
+        th_c = load_rows("th_c", th, nc.sync)
         n1_l = load_list("n1_l", n1)
-        n2_l = load_list("n2_l", n2)
-        n3_l = load_list("n3_l", n3)
         w_raw = keep.tile([P, PACK, H], F32)
         nc.sync.dma_start(w_raw[:], w1.rearrange("(p j) c -> p j c", j=PACK))
+        n2_l = load_list("n2_l", n2)
+        n3_l = load_list("n3_l", n3)
         n4_l = load_list("n4_l", n4)
         n5_l = load_list("n5_l", n5)
-        sl_c = load_rows("sl_c", sl, nc.gpsimd)
-        th_c = load_rows("th_c", th, nc.gpsimd)
+        x_table = load_words("x_table", x_words)
         gs_c = load_rows("gs_c", gs, nc.gpsimd)
+        bias_c = keep.tile([P, PACK], F32)
+        nc.vector.scalar_tensor_tensor(bias_c[:], sl_c[:], -1.0, th_c[:], ALU.mult, ALU.mult)
 
-        x_plane = keep.tile([P, S], U8, align_bytes=64)
-        nc.vector.memset(x_plane[:].bitcast(I32), 0)
-        x_picked = pick_scales("x", x_rows, offs_l, S)
-        move_rows(x_plane, x_picked)
-        x_table = load_words("x_rows_then_words", x_words)
-        for q in range(0, P, 32):
-            nc.vector.tensor_copy(x_plane[q : q + 1, :].bitcast(I32), x_picked[q : q + 1, :].bitcast(I32))
-        d_picked = pick_scales("d", d_rows, k1_l, H)
+        x_plane = pick_scales("x", x_rows, offs_l, S)
+        d_plane = pick_scales("d", d_rows, k1_l, H)
         d_table = load_words("d_rows_words_z", d_words)
-        d_plane = keep.tile([P, H], U8, align_bytes=64)
-        nc.vector.tensor_copy(d_plane[:].bitcast(I32), d_picked[:].bitcast(I32))
-        move_rows(d_plane, d_picked)
 
         w_bf = keep.tile([P, PACK, P, PACK], BF16, align_bytes=64)
         w_to = w_bf[:].rearrange("p t m j -> p m j t")
         w_from = w_raw[:].rearrange("p j (m t) -> p m j t", t=PACK)
-        nc.vector.tensor_copy(w_to[:, 0:64], w_from[:, 0:64])
-        nc.scalar.copy(w_to[:, 64:P], w_from[:, 64:P])
+        nc.vector.tensor_copy(w_to[:, 0:W_SPLIT], w_from[:, 0:W_SPLIT])
+        nc.scalar.copy(w_to[:, W_SPLIT:P], w_from[:, W_SPLIT:P])
         w_codes = keep.tile([P, H], U32, align_bytes=64)
         w_plane = keep.tile([P, H], U8, align_bytes=64)
         nc.vector.quantize_mx(w_codes[:].bitcast(FP8X4), w_plane[:], w_bf[:].rearrange("p t m j -> p (t m j)"))
@@ -99,10 +96,7 @@ def tile_picked_hdenseehppagtwo_none_p_kernel(
         x_codes = keep.tile([P, S], U32, align_bytes=64)
         nc.vector.tensor_copy(x_codes[:], x_table[:].bitcast(U32).indirect(offs_l[:]))
 
-        bias_c = keep.tile([P, PACK], F32)
-        nc.vector.scalar_tensor_tensor(bias_c[:], sl_c[:], -1.0, th_c[:], ALU.mult, ALU.mult)
-
-        u = keep.tile([P, PACK, S], F32)
+        y, sg = [], []
         for t in range(PACK):
             cols = slice(P * t, P * (t + 1))
             y_ps = psum.tile([P, S], F32, name=f"bank{t}")
@@ -110,26 +104,38 @@ def tile_picked_hdenseehppagtwo_none_p_kernel(
                 y_ps[:], lhsT=w_codes[:, cols].bitcast(FP8X4), lhsT_scale=w_plane[:, cols],
                 rhs=x_codes[:].bitcast(FP8X4), rhs_scale=x_plane[:], start=True, stop=True,
             )
-            y = keep.tile([P, S], F32, tag=f"y{t}")
-            nc.vector.tensor_copy(y[:], y_ps[:])
-            sg = keep.tile([P, S], F32, tag=f"sg{t}")
-            for lo in (0, S // 2):
+            width = S if t == PACK - 1 else 2 * S
+            y.append(keep.tile([P, width], F32, name=f"y{t}"))
+            if width > S:
+                nc.vector.memset(y[t][:, S:width], 0.0)
+            nc.vector.tensor_copy(y[t][:, 0:S], y_ps[:])
+
+        def pieces(t):
+            return ((0, S // 2), (S // 2, S)) if t == PACK - 1 else ((0, S),)
+
+        for t in range(PACK):
+            sg.append(keep.tile([P, S], F32, name=f"sg{t}"))
+            for lo, hi in pieces(t):
                 nc.scalar.activation(
-                    sg[:, lo : lo + S // 2], y[:].indirect(offsets(n1_l, lo, lo + S // 2)), ACT.Sigmoid,
+                    sg[t][:, lo:hi], y[t][:].indirect(offsets(n1_l, lo, hi)), ACT.Sigmoid,
                     bias=bias_c[:, t : t + 1], scale=sl_c[:, t : t + 1],
                 )
-            nc.vector.scalar_tensor_tensor(u[:, t, :], y[:], gs_c[:, t : t + 1], sg[:], ALU.mult, ALU.mult)
 
-        d_codes = keep.tile([P, H], U32, align_bytes=64)
-        for lo in (0, H // 2):
-            nc.vector.tensor_copy(
-                d_codes[:, lo : lo + H // 2], d_table[:].bitcast(U32).indirect(offsets(k1_l, lo, lo + H // 2))
-            )
+        u = keep.tile([P, PACK, S], F32)
+        d_codes = keep.tile([P, H], U32, name="w_codes", align_bytes=64)
+        for t in range(PACK):
+            for lo, hi in pieces(t):
+                nc.vector.scalar_tensor_tensor(
+                    u[:, t, lo:hi], y[t][:, lo:hi], gs_c[:, t : t + 1], sg[t][:, lo:hi], ALU.mult, ALU.mult
+                )
+            if t < 2:
+                lo, hi = t * H // 2, (t + 1) * H // 2
+                nc.vector.tensor_copy(d_codes[:, lo:hi], d_table[:].bitcast(U32).indirect(offsets(k1_l, lo, hi)))
 
         h = [keep.tile([P, S], F32, name=f"h{m}") for m in range(H // P)]
         for c, (lo, hi) in enumerate(CHUNKS):
             width = hi - lo
-            half = keep.tile([P, PACK, width], F32, tag=("half0", "sg3", "y3")[c])
+            half = keep.tile([P, PACK, width], F32, name=("half0", "sg3", "y3")[c])
             for s in range(lo, hi, 64):
                 for t in range(PACK):
                     nc.scalar.activation(
@@ -162,11 +168,10 @@ def tile_picked_hdenseehppagtwo_none_p_kernel(
                     nc.scalar.activation(page[m][:].indirect(offsets(lst, lo, hi)), h[m][:, lo:hi], ACT.Copy, scale=factor)
 
         def finish(m):
-            for lo in (0, U // 2):
-                hi = lo + U // 2
-                other = keep.tile([P, U // 2], F32, name=f"other{m}_{lo}")
+            for lo, hi in ((0, LAST), (LAST, U)):
+                other = keep.tile([P, hi - lo], F32, name=f"other{m}_{lo}")
                 nc.scalar.activation(other[:], page[m][:].indirect(offsets(n5_l, lo, hi)), ACT.Copy)
-                res = keep.tile([P, U // 2], F32, name=f"res{m}_{lo}")
+                res = keep.tile([P, hi - lo], F32, name=f"res{m}_{lo}")
                 nc.vector.tensor_tensor(res[:], page[m][:, lo:hi], other[:], ALU.subtract)
                 nc.sync.dma_start(out[P * m : P * (m + 1), lo:hi], res[:])
 

@@ -19,7 +19,7 @@ FLOPS = 2 * K * H * S * 2
 
 LAST = 352
 W_SPLIT = 80
-CHUNKS = ((0, 64), (64, 128), (128, 256))
+CHUNKS = ((0, 64), (64, 192), (192, 256))
 
 
 def offsets(lst, lo, hi):
@@ -52,6 +52,9 @@ def tile_picked_hdenseehppagtwo_none_p_kernel(
         def pick_scales(name, rows, lst, n):
             picked = keep.tile([P, n], U8, name=name + "_picked")
             nc.vector.tensor_copy(picked[:], rows[:].indirect(lst[:]))
+            return picked
+
+        def place_scales(name, picked, n):
             plane = keep.tile([P, n], U8, name=name + "_plane", align_bytes=64)
             nc.vector.tensor_copy(plane[:].bitcast(I32), picked[:].bitcast(I32))
             for a in range(1, 4):
@@ -72,17 +75,18 @@ def tile_picked_hdenseehppagtwo_none_p_kernel(
         w_raw = keep.tile([P, PACK, H], F32)
         nc.sync.dma_start(w_raw[:], w1.rearrange("(p j) c -> p j c", j=PACK))
         n2_l = load_list("n2_l", n2)
+        x_table = load_words("x_table", x_words)
         n3_l = load_list("n3_l", n3)
         n4_l = load_list("n4_l", n4)
         n5_l = load_list("n5_l", n5)
-        x_table = load_words("x_table", x_words)
         gs_c = load_rows("gs_c", gs, nc.gpsimd)
         bias_c = keep.tile([P, PACK], F32)
         nc.vector.scalar_tensor_tensor(bias_c[:], sl_c[:], -1.0, th_c[:], ALU.mult, ALU.mult)
 
-        x_plane = pick_scales("x", x_rows, offs_l, S)
-        d_plane = pick_scales("d", d_rows, k1_l, H)
+        x_plane = place_scales("x", pick_scales("x", x_rows, offs_l, S), S)
+        d_picked = pick_scales("d", d_rows, k1_l, H)
         d_table = load_words("d_rows_words_z", d_words)
+        d_plane = place_scales("d", d_picked, H)
 
         w_bf = keep.tile([P, PACK, P, PACK], BF16, align_bytes=64)
         w_to = w_bf[:].rearrange("p t m j -> p m j t")
@@ -121,18 +125,42 @@ def tile_picked_hdenseehppagtwo_none_p_kernel(
                     bias=bias_c[:, t : t + 1], scale=sl_c[:, t : t + 1],
                 )
 
+        def pick_d_codes(tag, pair):
+            codes = keep.tile([P, 2 * P], U32, tag=tag, align_bytes=64)
+            lo, hi = 2 * P * pair, 2 * P * (pair + 1)
+            nc.vector.tensor_copy(codes[:], d_table[:].bitcast(U32).indirect(offsets(k1_l, lo, hi)))
+            return codes
+
         u = keep.tile([P, PACK, S], F32)
-        d_codes = keep.tile([P, H], U32, name="w_codes", align_bytes=64)
+        d_codes = []
         for t in range(PACK):
             for lo, hi in pieces(t):
                 nc.vector.scalar_tensor_tensor(
                     u[:, t, lo:hi], y[t][:, lo:hi], gs_c[:, t : t + 1], sg[t][:, lo:hi], ALU.mult, ALU.mult
                 )
-            if t < 2:
-                lo, hi = t * H // 2, (t + 1) * H // 2
-                nc.vector.tensor_copy(d_codes[:, lo:hi], d_table[:].bitcast(U32).indirect(offsets(k1_l, lo, hi)))
+            if t == 0:
+                d_codes.append(pick_d_codes("w_codes", 0))
 
-        h = [keep.tile([P, S], F32, name=f"h{m}") for m in range(H // P)]
+        h = [keep.tile([P, 2, S], F32, name=f"h{pair}") for pair in range(2)]
+        quantised = []
+
+        def multiply(h_ps, pair, e, c):
+            m = 2 * pair + e
+            z_codes, z_plane = quantised[c]
+            nc.tensor.matmul_mx(
+                h_ps, lhsT=d_codes[pair][:, P * e : P * (e + 1)].bitcast(FP8X4),
+                lhsT_scale=d_plane[:, P * m : P * (m + 1)],
+                rhs=z_codes[:].bitcast(FP8X4), rhs_scale=z_plane[:], start=True, stop=True,
+            )
+
+        def make_h(bank, pair, chunks):
+            lo, hi = CHUNKS[chunks[0]][0], CHUNKS[chunks[-1]][1]
+            h_ps = psum.tile([P, 2, hi - lo], F32, name=f"bank{bank}")
+            for c in chunks:
+                for e in range(2):
+                    multiply(h_ps[:, e, CHUNKS[c][0] - lo : CHUNKS[c][1] - lo], pair, e, c)
+            nc.vector.tensor_scalar(h[pair][:, :, lo:hi], h_ps[:], 0.0625, None, ALU.mult)
+
         for c, (lo, hi) in enumerate(CHUNKS):
             width = hi - lo
             half = keep.tile([P, PACK, width], F32, name=("half0", "sg3", "y3")[c])
@@ -141,7 +169,7 @@ def tile_picked_hdenseehppagtwo_none_p_kernel(
                     nc.scalar.activation(
                         half[:, t, s - lo : s - lo + 64], u[:, t, :].indirect(offsets(n2_l, s, s + 64)), ACT.Copy, scale=0.5
                     )
-            z = keep.tile([P, width, PACK], BF16, tag="d_rows_words_z", align_bytes=64)
+            z = keep.tile([P, width, PACK], BF16, tag="z_then_d_codes" if c == 0 else "d_rows_words_z", align_bytes=64)
             nc.vector.tensor_tensor(
                 z[:].rearrange("p (a i) t -> p a t i", i=4),
                 u[:, :, lo:hi].rearrange("p t (a i) -> p a t i", i=4),
@@ -151,21 +179,24 @@ def tile_picked_hdenseehppagtwo_none_p_kernel(
             z_codes = keep.tile([P, width], U32, name=f"z_codes{c}", align_bytes=64)
             z_plane = keep.tile([P, width], U8, name=f"z_plane{c}", align_bytes=64)
             nc.vector.quantize_mx(z_codes[:].bitcast(FP8X4), z_plane[:], z[:].rearrange("p j t -> p (j t)"))
-            for m in range(H // P):
-                cols = slice(P * m, P * (m + 1))
-                h_ps = psum.tile([P, width], F32, name=f"bank{(4 * (c + 1) + m) % 8}")
-                nc.tensor.matmul_mx(
-                    h_ps[:], lhsT=d_codes[:, cols].bitcast(FP8X4), lhsT_scale=d_plane[:, cols],
-                    rhs=z_codes[:].bitcast(FP8X4), rhs_scale=z_plane[:], start=True, stop=True,
-                )
-                nc.vector.tensor_scalar(h[m][:, lo:hi], h_ps[:], 0.0625, None, ALU.mult)
+            quantised.append((z_codes, z_plane))
+            if c == 0:
+                for e in range(2):
+                    h_ps = psum.tile([P, width], F32, name=f"bank{4 + e}")
+                    multiply(h_ps[:], 0, e, c)
+                    nc.scalar.activation(h[0][:, e, lo:hi], h_ps[:], ACT.Copy, scale=0.0625)
+                d_codes.append(pick_d_codes("z_then_d_codes", 1))
+                make_h(6, 1, [c])
+            else:
+                make_h((6 + c) % 8, 0, [c])
+        make_h(1, 1, [1, 2])
 
         page = [keep.tile([P, U], F32, name=f"page{m}") for m in range(H // P)]
 
         def put(pair, lo, hi):
             for lst, factor in ((n3_l, 1.0), (n4_l, 0.5)):
                 for m in pair:
-                    nc.scalar.activation(page[m][:].indirect(offsets(lst, lo, hi)), h[m][:, lo:hi], ACT.Copy, scale=factor)
+                    nc.scalar.activation(page[m][:].indirect(offsets(lst, lo, hi)), h[m // 2][:, m % 2, lo:hi], ACT.Copy, scale=factor)
 
         def finish(m):
             for lo, hi in ((0, LAST), (LAST, U)):

@@ -161,14 +161,19 @@ def tile_picked_hdenseehppagtwo_none_p_kernel(
                     multiply(h_ps[:, e, CHUNKS[c][0] - lo : CHUNKS[c][1] - lo], pair, e, c)
             nc.vector.tensor_scalar(h[pair][:, :, lo:hi], h_ps[:], 0.0625, None, ALU.mult)
 
+        halves = []
         for c, (lo, hi) in enumerate(CHUNKS):
-            width = hi - lo
-            half = keep.tile([P, PACK, width], F32, name=("half0", "sg3", "y3")[c])
+            half = keep.tile([P, PACK, hi - lo], F32, name=("half0", "sg3", "y3")[c])
+            halves.append(half)
             for s in range(lo, hi, 64):
                 for t in range(PACK):
                     nc.scalar.activation(
                         half[:, t, s - lo : s - lo + 64], u[:, t, :].indirect(offsets(n2_l, s, s + 64)), ACT.Copy, scale=0.5
                     )
+
+        for c, (lo, hi) in enumerate(CHUNKS):
+            width = hi - lo
+            half = halves[c]
             z = keep.tile([P, width, PACK], BF16, tag="z_then_d_codes" if c == 0 else "d_rows_words_z", align_bytes=64)
             nc.vector.tensor_tensor(
                 z[:].rearrange("p (a i) t -> p a t i", i=4),

@@ -15,15 +15,18 @@ ACT = mybir.ActivationFunctionType
 K, T, S, H, U = 512, 2048, 256, 512, 512
 P = 128
 PACK = 4
-FLOPS = 2 * K * H * S * 2
+BLOCKS = K // 32
+PER_COLUMN = 16
+FLOPS = 2 * (2 * K * H * S)
 
-LAST = 352
 W_SPLIT = 80
 CHUNKS = ((0, 64), (64, 192), (192, 256))
+ST_STEP = 64
+OUT_SPLIT = 352
 
 
 def offsets(lst, lo, hi):
-    return lst[:, lo // 16 : hi // 16]
+    return lst[:, lo // PER_COLUMN : hi // PER_COLUMN]
 
 
 def tile_picked_hdenseehppagtwo_none_p_kernel(
@@ -39,10 +42,10 @@ def tile_picked_hdenseehppagtwo_none_p_kernel(
             nc.sync.dma_start(lst[:], src)
             return lst
 
-        def load_rows(name, src, queue):
-            col = keep.tile([P, PACK], F32, name=name)
-            queue.dma_start(col[:], src.rearrange("(p t) o -> p (t o)", t=PACK))
-            return col
+        def load_row_values(name, src, queue):
+            values = keep.tile([P, PACK], F32, name=name)
+            queue.dma_start(values[:], src.rearrange("(p t) o -> p (t o)", t=PACK))
+            return values
 
         def load_words(tag, src):
             words = keep.tile([P, T], I32, tag=tag, align_bytes=64)
@@ -55,22 +58,24 @@ def tile_picked_hdenseehppagtwo_none_p_kernel(
             return picked
 
         def place_scales(name, picked, n):
-            plane = keep.tile([P, n], U8, name=name + "_plane", align_bytes=64)
-            nc.vector.tensor_copy(plane[:].bitcast(I32), picked[:].bitcast(I32))
+            placed = keep.tile([P, n], U8, name=name + "_scale", align_bytes=64)
+            nc.vector.tensor_copy(placed[:].bitcast(I32), picked[:].bitcast(I32))
             for a in range(1, 4):
-                nc.sync.dma_start(plane[a:P:32, :].bitcast(I32), picked[8 * a : P : 32, :].bitcast(I32))
-            return plane
+                nc.sync.dma_start(placed[a:P:32, :].bitcast(I32), picked[8 * a : P : 32, :].bitcast(I32))
+            return placed
 
         offs_l = load_list("offs_l", offs)
         x_rows = keep.tile([P, T], U8)
-        nc.sync.dma_start(x_rows[:].bitcast(I32), x_scales[0].bitcast(I32).unsqueeze(1).to_broadcast([16, 8, T // 4]))
-        d_rows = keep.tile([P, T], U8, tag="d_rows_words_z", align_bytes=64)
+        nc.sync.dma_start(
+            x_rows[:].bitcast(I32), x_scales[0].bitcast(I32).unsqueeze(1).to_broadcast([BLOCKS, P // BLOCKS, T // 4])
+        )
+        d_rows = keep.tile([P, T], U8, tag="d_rows_then_words", align_bytes=64)
         nc.vector.memset(d_rows[:, 0 : T // 2].bitcast(I32), 0)
         nc.gpsimd.memset(d_rows[:, T // 2 : T].bitcast(I32), 0)
-        nc.sync.dma_start(d_rows[0:P:8, :].bitcast(I32), d_scales[0].bitcast(I32))
+        nc.sync.dma_start(d_rows[0 : P : P // BLOCKS, :].bitcast(I32), d_scales[0].bitcast(I32))
         k1_l = load_list("k1_l", k1)
-        sl_c = load_rows("sl_c", sl, nc.sync)
-        th_c = load_rows("th_c", th, nc.sync)
+        sl_c = load_row_values("sl_c", sl, nc.sync)
+        th_c = load_row_values("th_c", th, nc.sync)
         n1_l = load_list("n1_l", n1)
         w_raw = keep.tile([P, PACK, H], F32)
         nc.sync.dma_start(w_raw[:], w1.rearrange("(p j) c -> p j c", j=PACK))
@@ -79,43 +84,44 @@ def tile_picked_hdenseehppagtwo_none_p_kernel(
         n3_l = load_list("n3_l", n3)
         n4_l = load_list("n4_l", n4)
         n5_l = load_list("n5_l", n5)
-        gs_c = load_rows("gs_c", gs, nc.gpsimd)
+        gs_c = load_row_values("gs_c", gs, nc.gpsimd)
         bias_c = keep.tile([P, PACK], F32)
         nc.vector.scalar_tensor_tensor(bias_c[:], sl_c[:], -1.0, th_c[:], ALU.mult, ALU.mult)
 
-        x_plane = place_scales("x", pick_scales("x", x_rows, offs_l, S), S)
+        x_scale = place_scales("x", pick_scales("x", x_rows, offs_l, S), S)
         d_picked = pick_scales("d", d_rows, k1_l, H)
-        d_table = load_words("d_rows_words_z", d_words)
-        d_plane = place_scales("d", d_picked, H)
+        d_table = load_words("d_rows_then_words", d_words)
+        d_scale = place_scales("d", d_picked, H)
 
         w_bf = keep.tile([P, PACK, P, PACK], BF16, align_bytes=64)
         w_to = w_bf[:].rearrange("p t m j -> p m j t")
         w_from = w_raw[:].rearrange("p j (m t) -> p m j t", t=PACK)
         nc.vector.tensor_copy(w_to[:, 0:W_SPLIT], w_from[:, 0:W_SPLIT])
         nc.scalar.copy(w_to[:, W_SPLIT:P], w_from[:, W_SPLIT:P])
-        w_codes = keep.tile([P, H], U32, align_bytes=64)
-        w_plane = keep.tile([P, H], U8, align_bytes=64)
-        nc.vector.quantize_mx(w_codes[:].bitcast(FP8X4), w_plane[:], w_bf[:].rearrange("p t m j -> p (t m j)"))
+        w_codes = keep.tile([P, H], U32, tag="w_codes_then_d_codes", align_bytes=64)
+        w_scale = keep.tile([P, H], U8, align_bytes=64)
+        nc.vector.quantize_mx(w_codes[:].bitcast(FP8X4), w_scale[:], w_bf[:].rearrange("p t m j -> p (t m j)"))
 
         x_codes = keep.tile([P, S], U32, align_bytes=64)
         nc.vector.tensor_copy(x_codes[:], x_table[:].bitcast(U32).indirect(offs_l[:]))
 
+        last = PACK - 1
         y, sg = [], []
         for t in range(PACK):
             cols = slice(P * t, P * (t + 1))
             y_ps = psum.tile([P, S], F32, name=f"bank{t}")
             nc.tensor.matmul_mx(
-                y_ps[:], lhsT=w_codes[:, cols].bitcast(FP8X4), lhsT_scale=w_plane[:, cols],
-                rhs=x_codes[:].bitcast(FP8X4), rhs_scale=x_plane[:], start=True, stop=True,
+                y_ps[:], lhsT=w_codes[:, cols].bitcast(FP8X4), lhsT_scale=w_scale[:, cols],
+                rhs=x_codes[:].bitcast(FP8X4), rhs_scale=x_scale[:], start=True, stop=True,
             )
-            width = S if t == PACK - 1 else 2 * S
-            y.append(keep.tile([P, width], F32, name=f"y{t}"))
-            if width > S:
-                nc.vector.memset(y[t][:, S:width], 0.0)
+            window = S if t == last else 2 * S
+            y.append(keep.tile([P, window], F32, name=f"y{t}"))
+            if window > S:
+                nc.vector.memset(y[t][:, S:window], 0.0)
             nc.vector.tensor_copy(y[t][:, 0:S], y_ps[:])
 
         def pieces(t):
-            return ((0, S // 2), (S // 2, S)) if t == PACK - 1 else ((0, S),)
+            return ((0, S // 2), (S // 2, S)) if t == last else ((0, S),)
 
         for t in range(PACK):
             sg.append(keep.tile([P, S], F32, name=f"sg{t}"))
@@ -131,90 +137,89 @@ def tile_picked_hdenseehppagtwo_none_p_kernel(
             nc.vector.tensor_copy(codes[:], d_table[:].bitcast(U32).indirect(offsets(k1_l, lo, hi)))
             return codes
 
-        u = keep.tile([P, PACK, S], F32)
+        gst = keep.tile([P, PACK, S], F32)
         d_codes = []
         for t in range(PACK):
             for lo, hi in pieces(t):
                 nc.vector.scalar_tensor_tensor(
-                    u[:, t, lo:hi], y[t][:, lo:hi], gs_c[:, t : t + 1], sg[t][:, lo:hi], ALU.mult, ALU.mult
+                    gst[:, t, lo:hi], y[t][:, lo:hi], gs_c[:, t : t + 1], sg[t][:, lo:hi], ALU.mult, ALU.mult
                 )
             if t == 0:
-                d_codes.append(pick_d_codes("w_codes", 0))
+                d_codes.append(pick_d_codes("w_codes_then_d_codes", 0))
+
+        halves = []
+        for (lo, hi), tag in zip(CHUNKS, ("half_first", f"sg{last}", f"y{last}")):
+            half = keep.tile([P, PACK, hi - lo], F32, tag=tag)
+            halves.append(half)
+            for s in range(lo, hi, ST_STEP):
+                for t in range(PACK):
+                    nc.scalar.activation(
+                        half[:, t, s - lo : s - lo + ST_STEP],
+                        gst[:, t, :].indirect(offsets(n2_l, s, s + ST_STEP)),
+                        ACT.Copy, scale=0.5,
+                    )
 
         h = [keep.tile([P, 2, S], F32, name=f"h{pair}") for pair in range(2)]
-        quantised = []
+        z_codes, z_scale = [], []
 
-        def multiply(h_ps, pair, e, c):
-            m = 2 * pair + e
-            z_codes, z_plane = quantised[c]
-            nc.tensor.matmul_mx(
-                h_ps, lhsT=d_codes[pair][:, P * e : P * (e + 1)].bitcast(FP8X4),
-                lhsT_scale=d_plane[:, P * m : P * (m + 1)],
-                rhs=z_codes[:].bitcast(FP8X4), rhs_scale=z_plane[:], start=True, stop=True,
+        def quantise_z(c, z_tag, codes_tag, scale_tag):
+            lo, hi = CHUNKS[c]
+            z = keep.tile([P, hi - lo, PACK], BF16, tag=z_tag, align_bytes=64)
+            nc.vector.tensor_tensor(
+                z[:].rearrange("p (a i) t -> p a t i", i=4),
+                gst[:, :, lo:hi].rearrange("p t (a i) -> p a t i", i=4),
+                halves[c][:].rearrange("p t (a i) -> p a t i", i=4),
+                ALU.subtract,
             )
+            z_codes.append(keep.tile([P, hi - lo], U32, name=f"z_codes{c}", tag=codes_tag, align_bytes=64))
+            z_scale.append(keep.tile([P, hi - lo], U8, name=f"z_scale{c}", tag=scale_tag, align_bytes=64))
+            nc.vector.quantize_mx(z_codes[c][:].bitcast(FP8X4), z_scale[c][:], z[:].rearrange("p j t -> p (j t)"))
 
         def make_h(bank, pair, chunks):
             lo, hi = CHUNKS[chunks[0]][0], CHUNKS[chunks[-1]][1]
             h_ps = psum.tile([P, 2, hi - lo], F32, name=f"bank{bank}")
             for c in chunks:
                 for e in range(2):
-                    multiply(h_ps[:, e, CHUNKS[c][0] - lo : CHUNKS[c][1] - lo], pair, e, c)
+                    m = 2 * pair + e
+                    nc.tensor.matmul_mx(
+                        h_ps[:, e, CHUNKS[c][0] - lo : CHUNKS[c][1] - lo],
+                        lhsT=d_codes[pair][:, P * e : P * (e + 1)].bitcast(FP8X4),
+                        lhsT_scale=d_scale[:, P * m : P * (m + 1)],
+                        rhs=z_codes[c][:].bitcast(FP8X4), rhs_scale=z_scale[c][:], start=True, stop=True,
+                    )
             nc.vector.tensor_scalar(h[pair][:, :, lo:hi], h_ps[:], 0.0625, None, ALU.mult)
 
-        halves = []
-        for c, (lo, hi) in enumerate(CHUNKS):
-            half = keep.tile([P, PACK, hi - lo], F32, name=("half0", "sg3", "y3")[c])
-            halves.append(half)
-            for s in range(lo, hi, 64):
-                for t in range(PACK):
-                    nc.scalar.activation(
-                        half[:, t, s - lo : s - lo + 64], u[:, t, :].indirect(offsets(n2_l, s, s + 64)), ACT.Copy, scale=0.5
-                    )
-
-        for c, (lo, hi) in enumerate(CHUNKS):
-            width = hi - lo
-            half = halves[c]
-            z = keep.tile([P, width, PACK], BF16, tag="z_then_d_codes" if c == 0 else "d_rows_words_z", align_bytes=64)
-            nc.vector.tensor_tensor(
-                z[:].rearrange("p (a i) t -> p a t i", i=4),
-                u[:, :, lo:hi].rearrange("p t (a i) -> p a t i", i=4),
-                half[:].rearrange("p t (a i) -> p a t i", i=4),
-                ALU.subtract,
-            )
-            z_codes = keep.tile([P, width], U32, name=f"z_codes{c}", align_bytes=64)
-            z_plane = keep.tile([P, width], U8, name=f"z_plane{c}", align_bytes=64)
-            nc.vector.quantize_mx(z_codes[:].bitcast(FP8X4), z_plane[:], z[:].rearrange("p j t -> p (j t)"))
-            quantised.append((z_codes, z_plane))
-            if c == 0:
-                for e in range(2):
-                    h_ps = psum.tile([P, width], F32, name=f"bank{4 + e}")
-                    multiply(h_ps[:], 0, e, c)
-                    nc.scalar.activation(h[0][:, e, lo:hi], h_ps[:], ACT.Copy, scale=0.0625)
-                d_codes.append(pick_d_codes("z_then_d_codes", 1))
-                make_h(6, 1, [c])
-            else:
-                make_h((6 + c) % 8, 0, [c])
-        make_h(1, 1, [1, 2])
+        quantise_z(0, "z_then_d_codes", "codes_then_z", "scale_then_z")
+        make_h(4, 0, [0])
+        d_codes.append(pick_d_codes("z_then_d_codes", 1))
+        make_h(5, 1, [0])
+        quantise_z(1, "codes_then_z", "codes_middle", "scale_middle")
+        make_h(6, 0, [1])
+        quantise_z(2, "scale_then_z", "codes_last", "scale_last")
+        make_h(7, 0, [2])
+        make_h(0, 1, [1, 2])
 
         page = [keep.tile([P, U], F32, name=f"page{m}") for m in range(H // P)]
 
-        def put(pair, lo, hi):
+        def scatter(pair, lo, hi):
             for lst, factor in ((n3_l, 1.0), (n4_l, 0.5)):
-                for m in pair:
-                    nc.scalar.activation(page[m][:].indirect(offsets(lst, lo, hi)), h[m // 2][:, m % 2, lo:hi], ACT.Copy, scale=factor)
+                for e in range(2):
+                    nc.scalar.activation(
+                        page[2 * pair + e][:].indirect(offsets(lst, lo, hi)), h[pair][:, e, lo:hi], ACT.Copy, scale=factor
+                    )
 
         def finish(m):
-            for lo, hi in ((0, LAST), (LAST, U)):
+            for lo, hi in ((0, OUT_SPLIT), (OUT_SPLIT, U)):
                 other = keep.tile([P, hi - lo], F32, name=f"other{m}_{lo}")
                 nc.scalar.activation(other[:], page[m][:].indirect(offsets(n5_l, lo, hi)), ACT.Copy)
-                res = keep.tile([P, hi - lo], F32, name=f"res{m}_{lo}")
-                nc.vector.tensor_tensor(res[:], page[m][:, lo:hi], other[:], ALU.subtract)
-                nc.sync.dma_start(out[P * m : P * (m + 1), lo:hi], res[:])
+                result = keep.tile([P, hi - lo], F32, name=f"result{m}_{lo}")
+                nc.vector.tensor_tensor(result[:], page[m][:, lo:hi], other[:], ALU.subtract)
+                nc.sync.dma_start(out[P * m : P * (m + 1), lo:hi], result[:])
 
-        first = CHUNKS[0][1]
-        for pair in ((0, 1), (2, 3)):
-            put(pair, 0, first)
-        for pair in ((0, 1), (2, 3)):
-            put(pair, first, S)
-            for m in pair:
-                finish(m)
+        first_end = CHUNKS[0][1]
+        for pair in range(2):
+            scatter(pair, 0, first_end)
+        for pair in range(2):
+            scatter(pair, first_end, S)
+            for e in range(2):
+                finish(2 * pair + e)

from contextlib import ExitStack

import concourse.mybir as mybir

F32 = mybir.dt.float32
BF16 = mybir.dt.bfloat16
I32 = mybir.dt.int32
U32 = mybir.dt.uint32
U16 = mybir.dt.uint16
U8 = mybir.dt.uint8
FP8X4 = mybir.dt.float8_e4m3fn_x4
ALU = mybir.AluOpType
ACT = mybir.ActivationFunctionType

K, T, S, H, U = 512, 2048, 256, 512, 512
P = 128
PACK = 4
BLOCKS = K // 32
PER_COLUMN = 16
FLOPS = 2 * (2 * K * H * S)

W_SPLIT = 80
CHUNKS = ((0, 64), (64, 192), (192, 256))
ST_STEP = 64
OUT_SPLIT = 352


def offsets(lst, lo, hi):
    return lst[:, lo // PER_COLUMN : hi // PER_COLUMN]


def tile_picked_hdenseehppagtwo_none_p_kernel(
    tc, x_words, x_scales, w1, sl, th, gs, d_words, d_scales, offs, n1, n2, k1, n3, n4, n5, out
):
    nc = tc.nc
    with ExitStack() as ctx:
        keep = ctx.enter_context(tc.tile_pool(name="keep", bufs=1))
        psum = ctx.enter_context(tc.psum_pool(name="psum", bufs=1))

        def load_list(name, src):
            lst = keep.tile(list(src.shape), U16, name=name)
            nc.sync.dma_start(lst[:], src)
            return lst

        def load_row_values(name, src, queue):
            values = keep.tile([P, PACK], F32, name=name)
            queue.dma_start(values[:], src.rearrange("(p t) o -> p (t o)", t=PACK))
            return values

        def load_words(tag, src):
            words = keep.tile([P, T], I32, tag=tag, align_bytes=64)
            nc.sync.dma_start(words[:], src[0].rearrange("p n r -> p (n r)").bitcast(I32))
            return words

        def pick_scales(name, rows, lst, n):
            picked = keep.tile([P, n], U8, name=name + "_picked")
            nc.vector.tensor_copy(picked[:], rows[:].indirect(lst[:]))
            return picked

        def place_scales(name, picked, n):
            placed = keep.tile([P, n], U8, name=name + "_scale", align_bytes=64)
            nc.vector.tensor_copy(placed[:].bitcast(I32), picked[:].bitcast(I32))
            for a in range(1, 4):
                nc.sync.dma_start(placed[a:P:32, :].bitcast(I32), picked[8 * a : P : 32, :].bitcast(I32))
            return placed

        offs_l = load_list("offs_l", offs)
        x_rows = keep.tile([P, T], U8)
        nc.sync.dma_start(
            x_rows[:].bitcast(I32), x_scales[0].bitcast(I32).unsqueeze(1).to_broadcast([BLOCKS, P // BLOCKS, T // 4])
        )
        d_rows = keep.tile([P, T], U8, tag="d_rows_then_words", align_bytes=64)
        nc.vector.memset(d_rows[:, 0 : T // 2].bitcast(I32), 0)
        nc.gpsimd.memset(d_rows[:, T // 2 : T].bitcast(I32), 0)
        nc.sync.dma_start(d_rows[0 : P : P // BLOCKS, :].bitcast(I32), d_scales[0].bitcast(I32))
        k1_l = load_list("k1_l", k1)
        sl_c = load_row_values("sl_c", sl, nc.sync)
        th_c = load_row_values("th_c", th, nc.sync)
        n1_l = load_list("n1_l", n1)
        w_raw = keep.tile([P, PACK, H], F32)
        nc.sync.dma_start(w_raw[:], w1.rearrange("(p j) c -> p j c", j=PACK))
        n2_l = load_list("n2_l", n2)
        x_table = load_words("x_table", x_words)
        n3_l = load_list("n3_l", n3)
        n4_l = load_list("n4_l", n4)
        n5_l = load_list("n5_l", n5)
        gs_c = load_row_values("gs_c", gs, nc.gpsimd)
        bias_c = keep.tile([P, PACK], F32)
        nc.vector.scalar_tensor_tensor(bias_c[:], sl_c[:], -1.0, th_c[:], ALU.mult, ALU.mult)

        x_scale = place_scales("x", pick_scales("x", x_rows, offs_l, S), S)
        d_picked = pick_scales("d", d_rows, k1_l, H)
        d_table = load_words("d_rows_then_words", d_words)
        d_scale = place_scales("d", d_picked, H)

        w_bf = keep.tile([P, PACK, P, PACK], BF16, align_bytes=64)
        w_to = w_bf[:].rearrange("p t m j -> p m j t")
        w_from = w_raw[:].rearrange("p j (m t) -> p m j t", t=PACK)
        nc.vector.tensor_copy(w_to[:, 0:W_SPLIT], w_from[:, 0:W_SPLIT])
        nc.scalar.copy(w_to[:, W_SPLIT:P], w_from[:, W_SPLIT:P])
        w_codes = keep.tile([P, H], U32, tag="w_codes_then_d_codes", align_bytes=64)
        w_scale = keep.tile([P, H], U8, align_bytes=64)
        nc.vector.quantize_mx(w_codes[:].bitcast(FP8X4), w_scale[:], w_bf[:].rearrange("p t m j -> p (t m j)"))

        x_codes = keep.tile([P, S], U32, align_bytes=64)
        nc.vector.tensor_copy(x_codes[:], x_table[:].bitcast(U32).indirect(offs_l[:]))

        last = PACK - 1
        y, sg = [], []
        for t in range(PACK):
            cols = slice(P * t, P * (t + 1))
            y_ps = psum.tile([P, S], F32, name=f"bank{t}")
            nc.tensor.matmul_mx(
                y_ps[:], lhsT=w_codes[:, cols].bitcast(FP8X4), lhsT_scale=w_scale[:, cols],
                rhs=x_codes[:].bitcast(FP8X4), rhs_scale=x_scale[:], start=True, stop=True,
            )
            window = S if t == last else 2 * S
            y.append(keep.tile([P, window], F32, name=f"y{t}"))
            if window > S:
                nc.vector.memset(y[t][:, S:window], 0.0)
            nc.vector.tensor_copy(y[t][:, 0:S], y_ps[:])

        def pieces(t):
            return ((0, S // 2), (S // 2, S)) if t == last else ((0, S),)

        for t in range(PACK):
            sg.append(keep.tile([P, S], F32, name=f"sg{t}"))
            for lo, hi in pieces(t):
                nc.scalar.activation(
                    sg[t][:, lo:hi], y[t][:].indirect(offsets(n1_l, lo, hi)), ACT.Sigmoid,
                    bias=bias_c[:, t : t + 1], scale=sl_c[:, t : t + 1],
                )

        def pick_d_codes(tag, pair):
            codes = keep.tile([P, 2 * P], U32, tag=tag, align_bytes=64)
            lo, hi = 2 * P * pair, 2 * P * (pair + 1)
            nc.vector.tensor_copy(codes[:], d_table[:].bitcast(U32).indirect(offsets(k1_l, lo, hi)))
            return codes

        gst = keep.tile([P, PACK, S], F32)
        d_codes = []
        for t in range(PACK):
            for lo, hi in pieces(t):
                nc.vector.scalar_tensor_tensor(
                    gst[:, t, lo:hi], y[t][:, lo:hi], gs_c[:, t : t + 1], sg[t][:, lo:hi], ALU.mult, ALU.mult
                )
            if t == 0:
                d_codes.append(pick_d_codes("w_codes_then_d_codes", 0))

        halves = []
        for (lo, hi), tag in zip(CHUNKS, ("half_first", f"sg{last}", f"y{last}")):
            half = keep.tile([P, PACK, hi - lo], F32, tag=tag)
            halves.append(half)
            for s in range(lo, hi, ST_STEP):
                for t in range(PACK):
                    nc.scalar.activation(
                        half[:, t, s - lo : s - lo + ST_STEP],
                        gst[:, t, :].indirect(offsets(n2_l, s, s + ST_STEP)),
                        ACT.Copy, scale=0.5,
                    )

        h = [keep.tile([P, 2, S], F32, name=f"h{pair}") for pair in range(2)]
        z_codes, z_scale = [], []

        def quantise_z(c, z_tag, codes_tag, scale_tag):
            lo, hi = CHUNKS[c]
            z = keep.tile([P, hi - lo, PACK], BF16, tag=z_tag, align_bytes=64)
            nc.vector.tensor_tensor(
                z[:].rearrange("p (a i) t -> p a t i", i=4),
                gst[:, :, lo:hi].rearrange("p t (a i) -> p a t i", i=4),
                halves[c][:].rearrange("p t (a i) -> p a t i", i=4),
                ALU.subtract,
            )
            z_codes.append(keep.tile([P, hi - lo], U32, name=f"z_codes{c}", tag=codes_tag, align_bytes=64))
            z_scale.append(keep.tile([P, hi - lo], U8, name=f"z_scale{c}", tag=scale_tag, align_bytes=64))
            nc.vector.quantize_mx(z_codes[c][:].bitcast(FP8X4), z_scale[c][:], z[:].rearrange("p j t -> p (j t)"))

        def make_h(bank, pair, chunks):
            lo, hi = CHUNKS[chunks[0]][0], CHUNKS[chunks[-1]][1]
            h_ps = psum.tile([P, 2, hi - lo], F32, name=f"bank{bank}")
            for c in chunks:
                for e in range(2):
                    m = 2 * pair + e
                    nc.tensor.matmul_mx(
                        h_ps[:, e, CHUNKS[c][0] - lo : CHUNKS[c][1] - lo],
                        lhsT=d_codes[pair][:, P * e : P * (e + 1)].bitcast(FP8X4),
                        lhsT_scale=d_scale[:, P * m : P * (m + 1)],
                        rhs=z_codes[c][:].bitcast(FP8X4), rhs_scale=z_scale[c][:], start=True, stop=True,
                    )
            nc.vector.tensor_scalar(h[pair][:, :, lo:hi], h_ps[:], 0.0625, None, ALU.mult)

        quantise_z(0, "z_then_d_codes", "codes_then_z", "scale_then_z")
        make_h(4, 0, [0])
        d_codes.append(pick_d_codes("z_then_d_codes", 1))
        make_h(5, 1, [0])
        quantise_z(1, "codes_then_z", "codes_middle", "scale_middle")
        make_h(6, 0, [1])
        quantise_z(2, "scale_then_z", "codes_last", "scale_last")
        make_h(7, 0, [2])
        make_h(0, 1, [1, 2])

        page = [keep.tile([P, U], F32, name=f"page{m}") for m in range(H // P)]

        def scatter(pair, lo, hi):
            for lst, factor in ((n3_l, 1.0), (n4_l, 0.5)):
                for e in range(2):
                    nc.scalar.activation(
                        page[2 * pair + e][:].indirect(offsets(lst, lo, hi)), h[pair][:, e, lo:hi], ACT.Copy, scale=factor
                    )

        def finish(m):
            for lo, hi in ((0, OUT_SPLIT), (OUT_SPLIT, U)):
                other = keep.tile([P, hi - lo], F32, name=f"other{m}_{lo}")
                nc.scalar.activation(other[:], page[m][:].indirect(offsets(n5_l, lo, hi)), ACT.Copy)
                result = keep.tile([P, hi - lo], F32, name=f"result{m}_{lo}")
                nc.vector.tensor_tensor(result[:], page[m][:, lo:hi], other[:], ALU.subtract)
                nc.sync.dma_start(out[P * m : P * (m + 1), lo:hi], result[:])

        first_end = CHUNKS[0][1]
        for pair in range(2):
            scatter(pair, 0, first_end)
        for pair in range(2):
            scatter(pair, first_end, S)
            for e in range(2):
                finish(2 * pair + e)
